import numpy as np
import ml_dtypes


def mxq(x, axis, fmt="e4m3"):
    dtype, down = {"e4m3": (ml_dtypes.float8_e4m3fn, 7), "e5m2": (ml_dtypes.float8_e5m2, 14)}[fmt]
    v = np.moveaxis(np.asarray(x, np.float32).astype(ml_dtypes.bfloat16).astype(np.float64), axis, -1)
    blocks = v.reshape(v.shape[:-1] + (-1, 32))
    amax = np.abs(blocks).max(-1, keepdims=True)
    byte = np.maximum(np.where(amax > 0, np.frexp(amax)[1] - 1 + 127, 0) - down, 1)
    scale = np.exp2(byte - 127.0)
    codes = (blocks / scale).astype(np.float32).astype(dtype).astype(np.float64)
    return np.moveaxis((codes * scale).reshape(v.shape), -1, axis)


WIDE = False


def mx_kscale(k):
    if not WIDE:
        return np.ones(k)
    levels = np.array([10, -10, 5, -5, 0])
    if k % 512:
        return np.exp2(np.random.permutation(np.resize(levels, k // 32))).repeat(32)
    a = np.empty((k // 512, 16))
    for p in range(k // 512):
        a[p, :8] = np.random.permutation(np.resize(levels, 8))
        for g in range(8):
            far = levels[np.abs(levels - a[p, g]) >= 10]
            a[p, g + 8] = far[np.random.randint(len(far))]
    return np.exp2(a.ravel()).repeat(32)


def f64(x):
    return np.asarray(x).astype(np.float64)


def striped8(idx):
    return np.concatenate([x.reshape(-1, 16).T for x in idx]).astype(np.uint16)


def runs(offs, k):
    lists = np.stack([offs[16 * r : 16 * r + 16].T.reshape(-1) for r in range(8)]).astype(np.int64)
    return lists[np.arange(k) % 512 // 64]


def pack_weight(w):
    k, n = w.shape
    w = f64(np.asarray(w, np.float32).astype(ml_dtypes.bfloat16)).reshape(k // 32, 32, n)
    amax = np.abs(w).max(1)
    byte = np.clip(np.where(amax > 0, np.frexp(amax)[1] - 1 + 127 - 7, 1), 1, 254)
    scaled = (w * np.exp2(127.0 - byte)[:, None, :]).reshape(k, n).astype(np.float32)
    words = np.ascontiguousarray(scaled.reshape(k // 512, 128, 4, n).transpose(0, 1, 3, 2)).astype(ml_dtypes.float8_e4m3fn).view(np.uint8)
    return words, np.ascontiguousarray(byte.astype(np.uint8).reshape(k // 512, 16, n))


def unpack_weight(words, scales):
    g, p, n, _ = words.shape
    vals = np.ascontiguousarray(words).view(ml_dtypes.float8_e4m3fn).astype(np.float64) * np.repeat(np.exp2(scales.astype(np.float64) - 127.0), 8, axis=1)[..., None]
    return vals.transpose(0, 1, 3, 2).reshape(g * 512, n)


K, T, S, N, G, H = 512, 2048, 512, 512, 2048, 512


def setup_inputs():
    n = np.random.standard_normal
    s = mx_kscale(K)[:, None]
    u = mx_kscale(H)
    packed_xT = pack_weight(n((K, T)) * s)
    packed_dT = pack_weight(n((K, G)) / s)
    return {
        "x_words": packed_xT[0],
        "x_scales": packed_xT[1],
        "d_words": packed_dT[0],
        "d_scales": packed_dT[1],
        "gn": (np.random.uniform(0.5, 1.5, (H, 1)) * u[:, None]).astype(np.float32),
        "w1": (n((H, N)) / np.sqrt(H) / u[:, None]).astype(np.float32),
        "offs": striped8(np.random.randint(0, T, (8, S))),
        "kidx": striped8(np.random.randint(0, G, (8, H))),
        "nb": striped8(np.stack([np.random.permutation(S) for _ in range(8)])),
    }


def reference(x_words, x_scales, d_words, d_scales, gn, w1, offs, kidx, nb):
    d_kidx = unpack_weight(d_words, d_scales)[np.arange(K)[:, None], runs(kidx, K)]
    xq = unpack_weight(x_words, x_scales)[np.arange(K)[:, None], runs(offs, K)]
    s = 0.0625 * (d_kidx.T @ xq)
    z = f64(gn) * (np.tanh(np.maximum(s, s[np.arange(H)[:, None], runs(nb, H)])))
    return mxq(f64(w1), 0, "e4m3").T @ mxq(z, 0, "e4m3")

from contextlib import ExitStack

import concourse.mybir as mybir

K, T, S, N, G, H = 512, 2048, 512, 512, 2048, 512
FLOPS = 2 * K * H * S + 2 * H * N * S

F32 = mybir.dt.float32
BF16 = mybir.dt.bfloat16
I32 = mybir.dt.int32
U32 = mybir.dt.uint32
U16 = mybir.dt.uint16
U8 = mybir.dt.uint8
FP8X4 = mybir.dt.float8_e4m3fn_x4
ACT = mybir.ActivationFunctionType
ALU = mybir.AluOpType

P = 128
PACK = 4
CHUNKS = ((0, 256), (256, 128), (384, 128))
BANK = 512


def tile_picked_pqhash_tanh_p_kernel(tc, x_words, x_scales, d_words, d_scales, gn, w1, offs, kidx, nb, out):
    nc = tc.nc
    half = S // 2
    with ExitStack() as ctx:
        keep = ctx.enter_context(tc.tile_pool(name="keep", bufs=1))
        psum = ctx.enter_context(tc.psum_pool(name="psum", bufs=1))

        kidx_t = keep.tile([P, H // 16], U16, name="kidx_t")
        offs_t = keep.tile([P, S // 16], U16, name="offs_t")
        nb_t = keep.tile([P, S // 16], U16, name="nb_t")
        nc.sync.dma_start(kidx_t[:], kidx)
        nc.sync.dma_start(offs_t[:], offs)
        nc.sync.dma_start(nb_t[:], nb)
        gain = keep.tile([P, PACK], F32, name="gain")
        nc.sync.dma_start(gain[:], gn.rearrange("(p t) o -> p (t o)", t=PACK))

        d_byte_table = keep.tile([P, G], U8, name="d_byte_table", align_bytes=64)
        x_byte_table = keep.tile([P, T], U8, name="x_byte_table", align_bytes=64)
        for table, scales in ((x_byte_table, x_scales), (d_byte_table, d_scales)):
            nc.vector.memset(table[:].bitcast(I32), 0)
            nc.sync.dma_start(table[0:P:8, :].bitcast(I32), scales[0].bitcast(I32))

        d_word_table = keep.tile([P, G], U32, name="d_word_table", align_bytes=64)
        x_word_table = keep.tile([P, T], U32, name="x_word_table", align_bytes=64)
        nc.sync.dma_start(d_word_table[:].bitcast(I32), d_words[0].rearrange("p c r -> p (c r)").bitcast(I32))
        nc.sync.dma_start(x_word_table[:].bitcast(I32), x_words[0].rearrange("p c r -> p (c r)").bitcast(I32))

        d_bytes = keep.tile([P, H], U8, name="d_bytes", tag="early", align_bytes=64)
        x_bytes = keep.tile([P, S], U8, name="x_bytes", align_bytes=64)
        planes = keep.tile([P, H + S], U8, name="planes", align_bytes=64)
        d_plane = planes[:, 0:H]
        x_plane = planes[:, H : H + S]
        nc.vector.tensor_copy(x_bytes[:], x_byte_table[:].indirect(offs_t[:]))
        nc.vector.tensor_copy(d_bytes[:], d_byte_table[:].indirect(kidx_t[:]))
        nc.vector.tensor_copy(x_plane.bitcast(I32), x_bytes[:].bitcast(I32))
        nc.vector.tensor_copy(
            d_plane.rearrange("p (t m) -> p m t", t=PACK), d_bytes[:].rearrange("p (m t) -> p m t", t=PACK)
        )
        for j in range(1, 4):
            nc.sync.dma_start(planes[j:P:32, :].bitcast(I32), planes[8 * j : P : 32, :].bitcast(I32))

        w_rows = w1.rearrange("(p t) n -> p t n", t=PACK)
        w_raw = []
        for h in range(2):
            raw = keep.tile([P, PACK, N // 2], F32, name="w_raw%d" % h, tag=("w_raw0", "early")[h], align_bytes=64)
            nc.sync.dma_start(raw[:], w_rows[:, :, h * (N // 2) : (h + 1) * (N // 2)])
            w_raw.append(raw)

        d_picked = keep.tile([P, H], U32, name="d_picked", align_bytes=64)
        d_codes = keep.tile([P, H], U32, name="d_codes", align_bytes=64)
        nc.vector.tensor_copy(d_picked[:], d_word_table[:].indirect(kidx_t[:]))
        nc.vector.tensor_copy(
            d_codes[:].rearrange("p (t m) -> p m t", t=PACK), d_picked[:].rearrange("p (m t) -> p m t", t=PACK)
        )
        x_codes = []
        for h in range(2):
            codes = keep.tile([P, half], U32, name="x_codes%d" % h, align_bytes=64)
            nc.vector.tensor_copy(codes[:], x_word_table[:].indirect(offs_t[:, h * half // 16 : (h + 1) * half // 16]))
            x_codes.append(codes)

        th = [keep.tile([P, S], F32, name="th%d" % t) for t in range(PACK)]
        for pair in range(2):
            for h in range(2):
                cols = slice(h * half, (h + 1) * half)
                for t in (2 * pair, 2 * pair + 1):
                    keys = slice(t * P, (t + 1) * P)
                    acc = psum.tile([P, half], F32, name="score%d_%d" % (t, h), tag="bank%d" % (4 * pair + 2 * h + t % 2))
                    nc.tensor.matmul_mx(
                        out=acc[:],
                        lhsT=d_codes[:, keys].bitcast(FP8X4),
                        lhsT_scale=d_plane[:, keys],
                        rhs=x_codes[h][:].bitcast(FP8X4),
                        rhs_scale=x_plane[:, cols],
                        start=True,
                        stop=True,
                    )
                    nc.scalar.activation(th[t][:, cols], acc[:], ACT.Tanh, scale=0.0625)

        w_codes = keep.tile([P, N], U32, name="w_codes", align_bytes=64)
        w_plane = keep.tile([P, N], U8, name="w_plane", align_bytes=64)
        for h in range(2):
            grouped = keep.tile([P, N // 2 * PACK], BF16, name="w_grouped%d" % h, align_bytes=64)
            nc.vector.tensor_copy(
                grouped[:].rearrange("p (c i t) -> p c t i", i=4, t=PACK),
                w_raw[h][:].rearrange("p t (c i) -> p c t i", i=4),
            )
            cols = slice(h * (N // 2), (h + 1) * (N // 2))
            nc.vector.quantize_mx(out=w_codes[:, cols].bitcast(FP8X4), scales=w_plane[:, cols], in_=grouped[:])

        out_rows = out.rearrange("(mt p) j -> p mt j", p=P)
        bank_no = 0
        for ci, (j0, width) in enumerate(CHUNKS):
            picks = nb_t[:, j0 // 16 : (j0 + width) // 16]
            larger = keep.tile([P, PACK, width], F32, name="larger%d" % ci)
            for t in range(PACK):
                other = keep.tile([P, width], F32, name="other%d_%d" % (ci, t))
                if ci == 0 and t < 2:
                    nc.vector.tensor_copy(other[:], th[t][:].indirect(picks))
                else:
                    nc.scalar.activation(other[:], th[t][:].indirect(picks), ACT.Copy)
                nc.vector.tensor_tensor(larger[:, t, :], th[t][:, j0 : j0 + width], other[:], ALU.max)
            z = keep.tile([P, width * PACK], BF16, name="z%d" % ci, align_bytes=64)
            nc.vector.tensor_tensor(
                z[:].rearrange("p (c i t) -> p c t i", i=4, t=PACK),
                larger[:].rearrange("p t (c i) -> p c t i", i=4),
                gain[:].unsqueeze(1).unsqueeze(3).to_broadcast([P, width // 4, PACK, 4]),
                ALU.mult,
            )
            z_codes = keep.tile([P, width], U32, name="z_codes%d" % ci, align_bytes=64)
            z_plane = keep.tile([P, width], U8, name="z_plane%d" % ci, align_bytes=64)
            nc.vector.quantize_mx(out=z_codes[:].bitcast(FP8X4), scales=z_plane[:], in_=z[:])
            last = ci == len(CHUNKS) - 1
            per_bank = 2 if last else BANK // width
            for m0 in range(0, N // P, per_bank):
                acc = psum.tile([P, per_bank, width], F32, name="res%d" % bank_no, tag="bank%d" % bank_no)
                for g in range(per_bank):
                    cols = slice((m0 + g) * P, (m0 + g + 1) * P)
                    nc.tensor.matmul_mx(
                        out=acc[:, g, :],
                        lhsT=w_codes[:, cols].bitcast(FP8X4),
                        lhsT_scale=w_plane[:, cols],
                        rhs=z_codes[:].bitcast(FP8X4),
                        rhs_scale=z_plane[:],
                        start=True,
                        stop=True,
                    )
                staged = keep.tile([P, per_bank, width], F32, name="staged%d" % bank_no)
                if last and m0 == 0:
                    nc.vector.tensor_copy(staged[:], acc[:])
                else:
                    nc.scalar.copy(staged[:], acc[:])
                nc.sync.dma_start(out_rows[:, m0 : m0 + per_bank, j0 : j0 + width], staged[:])
                bank_no = bank_no + 1
